import numpy as np
import ml_dtypes


def mxq(x, axis, fmt="e4m3"):
    dtype, down = {"e4m3": (ml_dtypes.float8_e4m3fn, 7), "e5m2": (ml_dtypes.float8_e5m2, 14)}[fmt]
    v = np.moveaxis(np.asarray(x, np.float32).astype(ml_dtypes.bfloat16).astype(np.float64), axis, -1)
    blocks = v.reshape(v.shape[:-1] + (-1, 32))
    amax = np.abs(blocks).max(-1, keepdims=True)
    byte = np.maximum(np.where(amax > 0, np.frexp(amax)[1] - 1 + 127, 0) - down, 1)
    scale = np.exp2(byte - 127.0)
    codes = (blocks / scale).astype(np.float32).astype(dtype).astype(np.float64)
    return np.moveaxis((codes * scale).reshape(v.shape), -1, axis)


WIDE = False


def mx_kscale(k):
    if not WIDE:
        return np.ones(k)
    levels = np.array([10, -10, 5, -5, 0])
    if k % 512:
        return np.exp2(np.random.permutation(np.resize(levels, k // 32))).repeat(32)
    a = np.empty((k // 512, 16))
    for p in range(k // 512):
        a[p, :8] = np.random.permutation(np.resize(levels, 8))
        for g in range(8):
            far = levels[np.abs(levels - a[p, g]) >= 10]
            a[p, g + 8] = far[np.random.randint(len(far))]
    return np.exp2(a.ravel()).repeat(32)


def f64(x):
    return np.asarray(x).astype(np.float64)


def striped(idx):
    return np.tile(idx.reshape(-1, 16).T, (8, 1)).astype(np.uint16)


def unstriped(offs):
    return offs[:16].T.reshape(-1).astype(np.int64)


E2M1 = np.array([0.0, 0.5, 1.0, 1.5, 2.0, 3.0, 4.0, 6.0, -0.0, -0.5, -1.0, -1.5, -2.0, -3.0, -4.0, -6.0])


def pack_weight(w, fmt):
    k, n = w.shape
    w = f64(np.asarray(w, np.float32).astype(ml_dtypes.bfloat16)).reshape(k // 32, 32, n)
    amax = np.abs(w).max(1)
    if fmt == "e4m3":
        byte = np.frexp(amax)[1] - 1 + 127 - 7
    else:
        mant, ex = np.frexp(amax / 6.0)
        byte = np.where(mant > 0.5, ex, ex - 1) + 127
    byte = np.clip(np.where(amax > 0, byte, 1), 1, 254)
    scaled = (w * np.exp2(127.0 - byte)[:, None, :]).reshape(k, n).astype(np.float32)
    by_word = np.ascontiguousarray(scaled.reshape(k // 512, 128, 4, n).transpose(0, 1, 3, 2))
    if fmt == "e4m3":
        words = by_word.astype(ml_dtypes.float8_e4m3fn).view(np.uint8)
    else:
        c = by_word.astype(ml_dtypes.float4_e2m1fn).view(np.uint8) & 0xF
        words = (c[..., 0::2] | (c[..., 1::2] << 4)).reshape(k // 512, 128, 2 * n)
    return np.ascontiguousarray(words), np.ascontiguousarray(byte.astype(np.uint8).reshape(k // 512, 16, n))


def unpack_weight(words, scales, fmt):
    g, _, n = scales.shape
    words = np.ascontiguousarray(words).reshape(g, 128, n, -1)
    if fmt == "e4m3":
        vals = words.view(ml_dtypes.float8_e4m3fn).astype(np.float64)
    else:
        nib = np.empty((g, 128, n, 4), np.uint8)
        nib[..., 0::2] = words & 0xF
        nib[..., 1::2] = words >> 4
        vals = E2M1[nib]
    vals = vals * np.repeat(np.exp2(scales.astype(np.float64) - 127.0), 8, axis=1)[..., None]
    return vals.transpose(0, 1, 3, 2).reshape(g * 512, n)


def pack_table(v):
    words, scales = pack_weight(v, "e4m3")
    return np.concatenate([words.reshape(words.shape[0], -1), scales.reshape(scales.shape[0], -1)], axis=1)


def unpack_table(tab):
    g, t = tab.shape[0], tab.shape[1] // 528
    return unpack_weight(tab[:, :512 * t].reshape(g, 128, t, 4), tab[:, 512 * t:].reshape(g, 16, t), "e4m3")


def gelu(v):
    return 0.5 * v * (1.0 + np.tanh(np.sqrt(2.0 / np.pi) * (v + 0.044715 * v**3)))


K, M, T, S = 2048, 512, 2048, 512


def setup_inputs():
    n = np.random.standard_normal
    s = mx_kscale(K)[:, None]
    p_w4 = pack_weight(n((K, M)) / np.sqrt(K) / s, "e2m1")
    return {
        "tab": pack_table(n((K, T)) * s),
        "w4_words": p_w4[0],
        "w4_scales": p_w4[1],
        "dw": (0.3 * n((K, M)) / np.sqrt(K) / s).astype(np.float32),
        "b": (0.3 * n(512)).astype(np.float32),
        "offs": striped(np.random.permutation(T)[:S]),
    }


def reference(tab, w4_words, w4_scales, dw, b, offs):
    tab_ = unpack_table(tab)[:, unstriped(offs)]
    w4_ = unpack_weight(w4_words, w4_scales, "e2m1")
    dw_ = mxq(f64(dw), 0, "e4m3")
    y = w4_.T @ tab_ + dw_.T @ tab_
    return gelu(y + f64(b)[:, None])

@@ -1,0 +1,155 @@
+from contextlib import ExitStack
+
+import concourse.mybir as mybir
+from concourse.masks import make_identity
+
+K, M, T, S = 2048, 512, 2048, 512
+FLOPS = 2 * 2 * K * M * S
+
+F32 = mybir.dt.float32
+BF16 = mybir.dt.bfloat16
+I32 = mybir.dt.int32
+U32 = mybir.dt.uint32
+U16 = mybir.dt.uint16
+U8 = mybir.dt.uint8
+FP8X4 = mybir.dt.float8_e4m3fn_x4
+FP4X4 = mybir.dt.float4_e2m1fn_x4
+GELU = mybir.ActivationFunctionType.Gelu_apprx_tanh
+
+P = 128
+PASSES = K // 512
+MT = M // P
+LAST_CHUNKS = ((0, 256), (256, 384), (384, 512))
+
+
+def tile_list_tabd_gelu_kernel(tc, tab, w4_words, w4_scales, dw, b, offs, out):
+    nc = tc.nc
+    with ExitStack() as ctx:
+        keep = ctx.enter_context(tc.tile_pool(name="keep", bufs=1))
+        psum = ctx.enter_context(tc.psum_pool(name="psum", bufs=1))
+
+        offsets = keep.tile([P, S // 16], U16, name="offsets")
+        nc.sync.dma_start(offsets[:], offs)
+
+        w4s = keep.tile([P, PASSES, M], U8, name="w4s", align_bytes=64)
+        tabs = keep.tile([P, PASSES, T], U8, name="tabs", align_bytes=64)
+        nc.vector.memset(w4s[:].bitcast(I32), 0)
+        nc.vector.memset(tabs[:].bitcast(I32), 0)
+
+        warm = keep.tile([P, 1], F32, name="warm")
+        nc.gpsimd.memset(warm[:], 0.0)
+        warm_out = keep.tile([P, 1], F32, name="warm_out")
+        nc.scalar.activation(warm_out[:], warm[:], GELU)
+
+        raw = [keep.tile([P, 4, M], F32, name=f"raw{a}") for a in range(PASSES)]
+        words = [keep.tile([P, T], I32, name=f"words{a}") for a in range(PASSES)]
+        w4 = keep.tile([P, PASSES, 2 * M], U8, name="w4", align_bytes=64)
+
+        def load_dw(a, c0, c1):
+            nc.sync.dma_start(
+                raw[a][:, :, c0:c1],
+                dw[512 * a : 512 * (a + 1), c0:c1].rearrange("(p j) n -> p j n", j=4),
+            )
+
+        def load_words(a):
+            nc.sync.dma_start(words[a][:], tab[a, 0 : 512 * T].rearrange("(p n) -> p n", p=P).bitcast(I32))
+
+        load_dw(0, 0, M)
+        load_words(0)
+        nc.sync.dma_start(w4[:].bitcast(I32), w4_words.rearrange("a p n -> p a n").bitcast(I32))
+        for q in range(4):
+            nc.scalar.dma_start(
+                tabs[32 * q : 32 * q + 4, :, :].bitcast(I32),
+                tab[:, (512 + 4 * q) * T : (516 + 4 * q) * T].rearrange("a (r t) -> r a t", t=T).bitcast(I32),
+            )
+        for q in range(4):
+            nc.gpsimd.dma_start(
+                w4s[32 * q : 32 * q + 4, :, :].bitcast(I32),
+                w4_scales[:, 4 * q : 4 * q + 4, :].rearrange("a r n -> r a n").bitcast(I32),
+            )
+        brow = keep.tile([P, P], F32, name="brow")
+        nc.gpsimd.memset(brow[:], 0.0)
+        ident = keep.tile([P, P], F32, name="ident")
+        make_identity(nc, ident[:])
+        nc.gpsimd.dma_start(brow[0:MT, :], b.rearrange("(m p) -> m p", p=P))
+        bps = psum.tile([P, P], F32, name="bps")
+        bias = keep.tile([P, MT], F32, name="bias")
+
+        load_dw(1, 0, M)
+        load_words(1)
+        load_dw(2, 0, M)
+        load_words(2)
+        load_words(3)
+        for c0, c1 in LAST_CHUNKS:
+            load_dw(PASSES - 1, c0, c1)
+
+        gs = keep.tile([P, PASSES, S], U8, name="gs", align_bytes=64)
+
+        acc = [psum.tile([P, S], F32, name=f"acc{m}") for m in range(MT)]
+        dq = [keep.tile([P, M], U32, name=f"dq{a}", align_bytes=64) for a in range(PASSES)]
+        ds = [keep.tile([P, M], U8, name=f"ds{a}", align_bytes=64) for a in range(PASSES)]
+        bf = [keep.tile([P, M, 4], BF16, name=f"bf{a}", align_bytes=64) for a in range(PASSES)]
+        gw = [keep.tile([P, S], U32, name=f"gw{a}", align_bytes=64) for a in range(PASSES)]
+
+        def interleave(engine_copy, a, c0, c1):
+            engine_copy(bf[a][:, c0:c1, :], raw[a][:, :, c0:c1].rearrange("p j n -> p n j"))
+
+        def quantize(a, c0, c1):
+            nc.vector.quantize_mx(
+                out=dq[a][:, c0:c1].bitcast(FP8X4),
+                scales=ds[a][:, c0:c1],
+                in_=bf[a][:, c0:c1, :].rearrange("p n j -> p (n j)"),
+            )
+
+        def base_passes(a):
+            for m in range(MT):
+                nc.tensor.matmul_mx(
+                    out=acc[m][:],
+                    lhsT=w4[:, a, 256 * m : 256 * (m + 1)].bitcast(FP4X4),
+                    lhsT_scale=w4s[:, a, P * m : P * (m + 1)],
+                    rhs=gw[a][:].bitcast(FP8X4),
+                    rhs_scale=gs[:, a, :],
+                    start=(a == 0),
+                    stop=False,
+                )
+
+        def change_passes(a, ms):
+            for m in ms:
+                nc.tensor.matmul_mx(
+                    out=acc[m][:],
+                    lhsT=dq[a][:, P * m : P * (m + 1)].bitcast(FP8X4),
+                    lhsT_scale=ds[a][:, P * m : P * (m + 1)],
+                    rhs=gw[a][:].bitcast(FP8X4),
+                    rhs_scale=gs[:, a, :],
+                    start=False,
+                    stop=(a == PASSES - 1),
+                )
+
+        def finish(m):
+            res = keep.tile([P, S], F32, name=f"res{m}")
+            nc.scalar.activation(res[:], acc[m][:], GELU, bias=bias[:, m : m + 1])
+            nc.sync.dma_start(out[P * m : P * (m + 1), :], res[:])
+
+        for a in range(PASSES):
+            if a < PASSES - 1:
+                interleave(nc.scalar.copy, a, 0, M)
+            nc.vector.tensor_copy(gs[:, a, :], tabs[:, a, :].indirect(offsets[:]))
+            nc.vector.tensor_copy(gw[a][:], words[a][:].bitcast(U32).indirect(offsets[:]))
+            base_passes(a)
+            if a < PASSES - 1:
+                quantize(a, 0, M)
+                change_passes(a, range(MT))
+            if a == 1:
+                nc.tensor.transpose(bps[:], brow[:], ident[:])
+                nc.vector.tensor_copy(bias[:], bps[:, 0:MT])
+        a = PASSES - 1
+        for c0, c1 in LAST_CHUNKS:
+            cut = c0 + 80 if c0 == 0 else c0
+            if cut > c0:
+                interleave(nc.scalar.copy, a, c0, cut)
+            interleave(nc.vector.tensor_copy, a, cut, c1)
+            quantize(a, c0, c1)
+            ms = range(c0 // P, c1 // P)
+            change_passes(a, ms)
+            for m in ms:
+                finish(m)

@@ -19,7 +19,6 @@ GELU = mybir.ActivationFunctionType.Gelu_apprx_tanh
 P = 128
 PASSES = K // 512
 MT = M // P
-LAST_CHUNKS = ((0, 256), (256, 384), (384, 512))
 
 
 def tile_list_tabd_gelu_kernel(tc, tab, w4_words, w4_scales, dw, b, offs, out):
@@ -32,12 +31,17 @@ def tile_list_tabd_gelu_kernel(tc, tab, w4_words, w4_scales, dw, b, offs, out):
         nc.sync.dma_start(offsets[:], offs)
 
         w4s = keep.tile([P, PASSES, M], U8, name="w4s", align_bytes=64)
-        tabs = keep.tile([P, PASSES, T], U8, name="tabs", align_bytes=64)
-        nc.vector.memset(w4s[:].bitcast(I32), 0)
+        tabs = keep.tile([P, T], U8, name="tabs", align_bytes=64)
+        gp = keep.tile([P, S], U8, name="gp", align_bytes=64)
+        gs = keep.tile([P, PASSES - 1, S], U8, name="gs", align_bytes=64)
         nc.vector.memset(tabs[:].bitcast(I32), 0)
+        nc.vector.memset(w4s[:].bitcast(I32), 0)
+        nc.vector.memset(gs[:].bitcast(I32), 0)
 
         warm = keep.tile([P, 1], F32, name="warm")
         nc.gpsimd.memset(warm[:], 0.0)
+        brow = keep.tile([P, P], F32, name="brow")
+        nc.gpsimd.memset(brow[:], 0.0)
         warm_out = keep.tile([P, 1], F32, name="warm_out")
         nc.scalar.activation(warm_out[:], warm[:], GELU)
 
@@ -59,16 +63,14 @@ def tile_list_tabd_gelu_kernel(tc, tab, w4_words, w4_scales, dw, b, offs, out):
         nc.sync.dma_start(w4[:].bitcast(I32), w4_words.rearrange("a p n -> p a n").bitcast(I32))
         for q in range(4):
             nc.scalar.dma_start(
-                tabs[32 * q : 32 * q + 4, :, :].bitcast(I32),
-                tab[:, (512 + 4 * q) * T : (516 + 4 * q) * T].rearrange("a (r t) -> r a t", t=T).bitcast(I32),
+                tabs[32 * q : 32 * q + 16, :].bitcast(I32),
+                tab[:, (512 + 4 * q) * T : (516 + 4 * q) * T].rearrange("a (r t) -> a r t", t=T).bitcast(I32),
             )
         for q in range(4):
             nc.gpsimd.dma_start(
-                w4s[32 * q : 32 * q + 4, :, :].bitcast(I32),
-                w4_scales[:, 4 * q : 4 * q + 4, :].rearrange("a r n -> r a n").bitcast(I32),
+                w4s[q:P:32, :, :].bitcast(I32),
+                w4_scales[:, q:16:4, :].rearrange("a r n -> r a n").bitcast(I32),
             )
-        brow = keep.tile([P, P], F32, name="brow")
-        nc.gpsimd.memset(brow[:], 0.0)
         ident = keep.tile([P, P], F32, name="ident")
         make_identity(nc, ident[:])
         nc.gpsimd.dma_start(brow[0:MT, :], b.rearrange("(m p) -> m p", p=P))
@@ -80,10 +82,16 @@ def tile_list_tabd_gelu_kernel(tc, tab, w4_words, w4_scales, dw, b, offs, out):
         load_dw(2, 0, M)
         load_words(2)
         load_words(3)
-        for c0, c1 in LAST_CHUNKS:
-            load_dw(PASSES - 1, c0, c1)
+        load_dw(3, 0, 256)
+        load_dw(3, 256, 512)
 
-        gs = keep.tile([P, PASSES, S], U8, name="gs", align_bytes=64)
+        nc.vector.tensor_copy(gp[:], tabs[:].indirect(offsets[:]))
+        for a in range(1, PASSES):
+            for q in range(4):
+                nc.gpsimd.dma_start(
+                    gs[q:P:32, a - 1, :].bitcast(I32),
+                    gp[4 * a + q : P : 32, :].bitcast(I32),
+                )
 
         acc = [psum.tile([P, S], F32, name=f"acc{m}") for m in range(MT)]
         dq = [keep.tile([P, M], U32, name=f"dq{a}", align_bytes=64) for a in range(PASSES)]
@@ -108,7 +116,7 @@ def tile_list_tabd_gelu_kernel(tc, tab, w4_words, w4_scales, dw, b, offs, out):
                     lhsT=w4[:, a, 256 * m : 256 * (m + 1)].bitcast(FP4X4),
                     lhsT_scale=w4s[:, a, P * m : P * (m + 1)],
                     rhs=gw[a][:].bitcast(FP8X4),
-                    rhs_scale=gs[:, a, :],
+                    rhs_scale=gp[:] if a == 0 else gs[:, a - 1, :],
                     start=(a == 0),
                     stop=False,
                 )
@@ -120,7 +128,7 @@ def tile_list_tabd_gelu_kernel(tc, tab, w4_words, w4_scales, dw, b, offs, out):
                     lhsT=dq[a][:, P * m : P * (m + 1)].bitcast(FP8X4),
                     lhsT_scale=ds[a][:, P * m : P * (m + 1)],
                     rhs=gw[a][:].bitcast(FP8X4),
-                    rhs_scale=gs[:, a, :],
+                    rhs_scale=gp[4 * a : P, :],
                     start=False,
                     stop=(a == PASSES - 1),
                 )
@@ -133,7 +141,6 @@ def tile_list_tabd_gelu_kernel(tc, tab, w4_words, w4_scales, dw, b, offs, out):
         for a in range(PASSES):
             if a < PASSES - 1:
                 interleave(nc.scalar.copy, a, 0, M)
-            nc.vector.tensor_copy(gs[:, a, :], tabs[:, a, :].indirect(offsets[:]))
             nc.vector.tensor_copy(gw[a][:], words[a][:].bitcast(U32).indirect(offsets[:]))
             base_passes(a)
             if a < PASSES - 1:
@@ -143,13 +150,11 @@ def tile_list_tabd_gelu_kernel(tc, tab, w4_words, w4_scales, dw, b, offs, out):
                 nc.tensor.transpose(bps[:], brow[:], ident[:])
                 nc.vector.tensor_copy(bias[:], bps[:, 0:MT])
         a = PASSES - 1
-        for c0, c1 in LAST_CHUNKS:
-            cut = c0 + 80 if c0 == 0 else c0
-            if cut > c0:
-                interleave(nc.scalar.copy, a, c0, cut)
-            interleave(nc.vector.tensor_copy, a, cut, c1)
-            quantize(a, c0, c1)
-            ms = range(c0 // P, c1 // P)
-            change_passes(a, ms)
-            for m in ms:
-                finish(m)
+        for h in range(2):
+            c0 = 256 * h
+            interleave(nc.scalar.copy, a, c0, c0 + 80)
+            interleave(nc.vector.tensor_copy, a, c0 + 80, c0 + 256)
+            quantize(a, c0, c0 + 256)
+            change_passes(a, (2 * h, 2 * h + 1))
+            finish(2 * h)
+            finish(2 * h + 1)

@@ -1,7 +1,6 @@
 from contextlib import ExitStack
 
 import concourse.mybir as mybir
-from concourse.masks import make_identity
 
 K, M, T, S = 2048, 512, 2048, 512
 FLOPS = 2 * 2 * K * M * S
@@ -39,9 +38,10 @@ def tile_list_tabd_gelu_kernel(tc, tab, w4_words, w4_scales, dw, b, offs, out):
         nc.vector.memset(gs[:].bitcast(I32), 0)
 
         warm = keep.tile([P, 1], F32, name="warm")
-        nc.gpsimd.memset(warm[:], 0.0)
-        brow = keep.tile([P, P], F32, name="brow")
-        nc.gpsimd.memset(brow[:], 0.0)
+        nc.vector.memset(warm[:], 0.0)
+        brow = keep.tile([P, 32], F32, name="brow", align_bytes=64)
+        bias = keep.tile([P, 32], F32, name="bias", align_bytes=64)
+        nc.vector.memset(brow[:], 0.0)
         warm_out = keep.tile([P, 1], F32, name="warm_out")
         nc.scalar.activation(warm_out[:], warm[:], GELU)
 
@@ -58,40 +58,37 @@ def tile_list_tabd_gelu_kernel(tc, tab, w4_words, w4_scales, dw, b, offs, out):
         def load_words(a):
             nc.sync.dma_start(words[a][:], tab[a, 0 : 512 * T].rearrange("(p n) -> p n", p=P).bitcast(I32))
 
-        load_dw(0, 0, M)
-        load_words(0)
-        nc.sync.dma_start(w4[:].bitcast(I32), w4_words.rearrange("a p n -> p a n").bitcast(I32))
         for q in range(4):
             nc.scalar.dma_start(
                 tabs[32 * q : 32 * q + 16, :].bitcast(I32),
                 tab[:, (512 + 4 * q) * T : (516 + 4 * q) * T].rearrange("a (r t) -> a r t", t=T).bitcast(I32),
             )
-        for q in range(4):
+        for r in range(4):
             nc.gpsimd.dma_start(
-                w4s[q:P:32, :, :].bitcast(I32),
-                w4_scales[:, q:16:4, :].rearrange("a r n -> r a n").bitcast(I32),
+                w4s[r:P:32, :, :].bitcast(I32),
+                w4_scales[:, r:16:4, :].rearrange("a r n -> r a n").bitcast(I32),
             )
-        ident = keep.tile([P, P], F32, name="ident")
-        make_identity(nc, ident[:])
-        nc.gpsimd.dma_start(brow[0:MT, :], b.rearrange("(m p) -> m p", p=P))
-        bps = psum.tile([P, P], F32, name="bps")
-        bias = keep.tile([P, MT], F32, name="bias")
-
+        load_dw(0, 0, M)
+        load_words(0)
+        nc.sync.dma_start(w4[:].bitcast(I32), w4_words.rearrange("a p n -> p a n").bitcast(I32))
         load_dw(1, 0, M)
         load_words(1)
-        load_dw(2, 0, M)
         load_words(2)
-        load_words(3)
-        load_dw(3, 0, 256)
-        load_dw(3, 256, 512)
+
+        def shift(engine, a):
+            for r in range(4):
+                engine.dma_start(gs[r:P:32, a - 1, :].bitcast(I32), gp[4 * a + r : P : 32, :].bitcast(I32))
 
         nc.vector.tensor_copy(gp[:], tabs[:].indirect(offsets[:]))
-        for a in range(1, PASSES):
-            for q in range(4):
-                nc.gpsimd.dma_start(
-                    gs[q:P:32, a - 1, :].bitcast(I32),
-                    gp[4 * a + q : P : 32, :].bitcast(I32),
-                )
+        shift(nc.scalar, 1)
+        shift(nc.gpsimd, 2)
+        shift(nc.gpsimd, 3)
+        load_words(3)
+        load_dw(2, 0, M)
+        for m in range(MT):
+            nc.sync.dma_start(brow[m:P:32, :], b[P * m : P * (m + 1)].rearrange("(q i) -> q i", i=32))
+        load_dw(3, 0, 256)
+        load_dw(3, 256, 512)
 
         acc = [psum.tile([P, S], F32, name=f"acc{m}") for m in range(MT)]
         dq = [keep.tile([P, M], U32, name=f"dq{a}", align_bytes=64) for a in range(PASSES)]
@@ -138,23 +135,38 @@ def tile_list_tabd_gelu_kernel(tc, tab, w4_words, w4_scales, dw, b, offs, out):
             nc.scalar.activation(res[:], acc[m][:], GELU, bias=bias[:, m : m + 1])
             nc.sync.dma_start(out[P * m : P * (m + 1), :], res[:])
 
-        for a in range(PASSES):
-            if a < PASSES - 1:
-                interleave(nc.scalar.copy, a, 0, M)
+        def gather_words(a):
             nc.vector.tensor_copy(gw[a][:], words[a][:].bitcast(U32).indirect(offsets[:]))
-            base_passes(a)
-            if a < PASSES - 1:
-                quantize(a, 0, M)
-                change_passes(a, range(MT))
-            if a == 1:
-                nc.tensor.transpose(bps[:], brow[:], ident[:])
-                nc.vector.tensor_copy(bias[:], bps[:, 0:MT])
-        a = PASSES - 1
-        for h in range(2):
-            c0 = 256 * h
-            interleave(nc.scalar.copy, a, c0, c0 + 80)
-            interleave(nc.vector.tensor_copy, a, c0 + 80, c0 + 256)
-            quantize(a, c0, c0 + 256)
-            change_passes(a, (2 * h, 2 * h + 1))
-            finish(2 * h)
-            finish(2 * h + 1)
+
+        interleave(nc.scalar.copy, 0, 0, M)
+        gather_words(0)
+        base_passes(0)
+        quantize(0, 0, M)
+        change_passes(0, range(MT))
+
+        interleave(nc.scalar.copy, 1, 0, M)
+
+        gather_words(1)
+        quantize(1, 0, M)
+        change_passes(1, range(MT))
+        base_passes(1)
+        gather_words(2)
+        base_passes(2)
+        gather_words(3)
+        base_passes(3)
+
+        interleave(nc.scalar.copy, 2, 0, 192)
+        interleave(nc.vector.tensor_copy, 2, 192, M)
+        quantize(2, 0, M)
+        change_passes(2, range(MT))
+
+        for c0, c1 in ((0, 256), (256, 512)):
+            interleave(nc.scalar.copy, 3, c0, c0 + 80)
+            interleave(nc.vector.tensor_copy, 3, c0 + 80, c1)
+            quantize(3, c0, c1)
+            if c0 == 0:
+                nc.vector.transpose(bias[:], brow[:])
+            ms = range(c0 // P, c1 // P)
+            change_passes(3, ms)
+            for m in ms:
+                finish(m)

@@ -18,6 +18,7 @@ GELU = mybir.ActivationFunctionType.Gelu_apprx_tanh
 P = 128
 PASSES = K // 512
 MT = M // P
+TAIL = ((2, 0, 256, 128), (3, 0, 256, 128), (2, 256, 512, 384), (3, 256, 384, 256), (3, 384, 512, 384))
 
 
 def tile_list_tabd_gelu_kernel(tc, tab, w4_words, w4_scales, dw, b, offs, out):
@@ -27,7 +28,6 @@ def tile_list_tabd_gelu_kernel(tc, tab, w4_words, w4_scales, dw, b, offs, out):
         psum = ctx.enter_context(tc.psum_pool(name="psum", bufs=1))
 
         offsets = keep.tile([P, S // 16], U16, name="offsets")
-        nc.sync.dma_start(offsets[:], offs)
 
         w4s = keep.tile([P, PASSES, M], U8, name="w4s", align_bytes=64)
         tabs = keep.tile([P, T], U8, name="tabs", align_bytes=64)
@@ -63,12 +63,15 @@ def tile_list_tabd_gelu_kernel(tc, tab, w4_words, w4_scales, dw, b, offs, out):
                 tabs[32 * q : 32 * q + 16, :].bitcast(I32),
                 tab[:, (512 + 4 * q) * T : (516 + 4 * q) * T].rearrange("a (r t) -> a r t", t=T).bitcast(I32),
             )
-        for r in range(4):
+        for q in range(4):
             nc.gpsimd.dma_start(
-                w4s[r:P:32, :, :].bitcast(I32),
-                w4_scales[:, r:16:4, :].rearrange("a r n -> r a n").bitcast(I32),
+                w4s[32 * q : 32 * q + 4, :, :].bitcast(I32),
+                w4_scales[:, 4 * q : 4 * q + 4, :].rearrange("a r n -> r a n").bitcast(I32),
             )
+        for q in range(4):
+            nc.gpsimd.dma_start(brow[32 * q : 32 * q + MT, :], b.rearrange("(m q i) -> q m i", q=4, i=32)[q, :, :])
         load_dw(0, 0, M)
+        nc.sync.dma_start(offsets[:], offs)
         load_words(0)
         nc.sync.dma_start(w4[:].bitcast(I32), w4_words.rearrange("a p n -> p a n").bitcast(I32))
         load_dw(1, 0, M)
@@ -76,19 +79,22 @@ def tile_list_tabd_gelu_kernel(tc, tab, w4_words, w4_scales, dw, b, offs, out):
         load_words(2)
 
         def shift(engine, a):
-            for r in range(4):
-                engine.dma_start(gs[r:P:32, a - 1, :].bitcast(I32), gp[4 * a + r : P : 32, :].bitcast(I32))
+            for q in range(4):
+                engine.dma_start(
+                    gs[32 * q : 32 * q + 4, a - 1, :].bitcast(I32),
+                    gp[32 * q + 4 * a : 32 * q + 4 * a + 4, :].bitcast(I32),
+                )
 
         nc.vector.tensor_copy(gp[:], tabs[:].indirect(offsets[:]))
         shift(nc.scalar, 1)
         shift(nc.gpsimd, 2)
         shift(nc.gpsimd, 3)
         load_words(3)
-        load_dw(2, 0, M)
-        for m in range(MT):
-            nc.sync.dma_start(brow[m:P:32, :], b[P * m : P * (m + 1)].rearrange("(q i) -> q i", i=32))
+        load_dw(2, 0, 256)
         load_dw(3, 0, 256)
-        load_dw(3, 256, 512)
+        load_dw(2, 256, 512)
+        load_dw(3, 256, 384)
+        load_dw(3, 384, 512)
 
         acc = [psum.tile([P, S], F32, name=f"acc{m}") for m in range(MT)]
         dq = [keep.tile([P, M], U32, name=f"dq{a}", align_bytes=64) for a in range(PASSES)]
@@ -145,6 +151,7 @@ def tile_list_tabd_gelu_kernel(tc, tab, w4_words, w4_scales, dw, b, offs, out):
         change_passes(0, range(MT))
 
         interleave(nc.scalar.copy, 1, 0, M)
+        nc.vector.transpose(bias[:], brow[:])
 
         gather_words(1)
         quantize(1, 0, M)
@@ -155,18 +162,16 @@ def tile_list_tabd_gelu_kernel(tc, tab, w4_words, w4_scales, dw, b, offs, out):
         gather_words(3)
         base_passes(3)
 
-        interleave(nc.scalar.copy, 2, 0, 192)
-        interleave(nc.vector.tensor_copy, 2, 192, M)
-        quantize(2, 0, M)
-        change_passes(2, range(MT))
-
-        for c0, c1 in ((0, 256), (256, 512)):
-            interleave(nc.scalar.copy, 3, c0, c0 + 80)
-            interleave(nc.vector.tensor_copy, 3, c0 + 80, c1)
-            quantize(3, c0, c1)
-            if c0 == 0:
-                nc.vector.transpose(bias[:], brow[:])
+        for a, c0, c1, cut in TAIL:
+            if cut > c0:
+                interleave(nc.scalar.copy, a, c0, cut)
+            interleave(nc.vector.tensor_copy, a, cut, c1)
+            quantize(a, c0, c1)
+            if (a, c0) == (2, 256):
+                finish(0)
+                finish(1)
             ms = range(c0 // P, c1 // P)
-            change_passes(3, ms)
-            for m in ms:
-                finish(m)
+            change_passes(a, ms)
+            if a == PASSES - 1 and c0 >= 256:
+                for m in ms:
+                    finish(m)

from contextlib import ExitStack

import concourse.mybir as mybir

K, M, T, S = 2048, 512, 2048, 512
FLOPS = 2 * 2 * K * M * S

F32 = mybir.dt.float32
BF16 = mybir.dt.bfloat16
I32 = mybir.dt.int32
U32 = mybir.dt.uint32
U16 = mybir.dt.uint16
U8 = mybir.dt.uint8
FP8X4 = mybir.dt.float8_e4m3fn_x4
FP4X4 = mybir.dt.float4_e2m1fn_x4
GELU = mybir.ActivationFunctionType.Gelu_apprx_tanh

P = 128
PASSES = K // 512
MT = M // P
TAIL = ((2, 0, 256, 128), (3, 0, 256, 128), (2, 256, 512, 384), (3, 256, 384, 256), (3, 384, 512, 384))


def tile_list_tabd_gelu_kernel(tc, tab, w4_words, w4_scales, dw, b, offs, out):
    nc = tc.nc
    with ExitStack() as ctx:
        keep = ctx.enter_context(tc.tile_pool(name="keep", bufs=1))
        psum = ctx.enter_context(tc.psum_pool(name="psum", bufs=1))

        offsets = keep.tile([P, S // 16], U16, name="offsets")

        w4s = keep.tile([P, PASSES, M], U8, name="w4s", align_bytes=64)
        tabs = keep.tile([P, T], U8, name="tabs", align_bytes=64)
        gp = keep.tile([P, S], U8, name="gp", align_bytes=64)
        gs = keep.tile([P, PASSES - 1, S], U8, name="gs", align_bytes=64)
        nc.vector.memset(tabs[:].bitcast(I32), 0)
        nc.vector.memset(w4s[:].bitcast(I32), 0)
        nc.vector.memset(gs[:].bitcast(I32), 0)

        warm = keep.tile([P, 1], F32, name="warm")
        nc.vector.memset(warm[:], 0.0)
        brow = keep.tile([P, 32], F32, name="brow", align_bytes=64)
        bias = keep.tile([P, 32], F32, name="bias", align_bytes=64)
        nc.vector.memset(brow[:], 0.0)
        warm_out = keep.tile([P, 1], F32, name="warm_out")
        nc.scalar.activation(warm_out[:], warm[:], GELU)

        raw = [keep.tile([P, 4, M], F32, name=f"raw{a}") for a in range(PASSES)]
        words = [keep.tile([P, T], I32, name=f"words{a}") for a in range(PASSES)]
        w4 = keep.tile([P, PASSES, 2 * M], U8, name="w4", align_bytes=64)

        def load_dw(a, c0, c1):
            nc.sync.dma_start(
                raw[a][:, :, c0:c1],
                dw[512 * a : 512 * (a + 1), c0:c1].rearrange("(p j) n -> p j n", j=4),
            )

        def load_words(a):
            nc.sync.dma_start(words[a][:], tab[a, 0 : 512 * T].rearrange("(p n) -> p n", p=P).bitcast(I32))

        for q in range(4):
            nc.scalar.dma_start(
                tabs[32 * q : 32 * q + 16, :].bitcast(I32),
                tab[:, (512 + 4 * q) * T : (516 + 4 * q) * T].rearrange("a (r t) -> a r t", t=T).bitcast(I32),
            )
        for q in range(4):
            nc.gpsimd.dma_start(
                w4s[32 * q : 32 * q + 4, :, :].bitcast(I32),
                w4_scales[:, 4 * q : 4 * q + 4, :].rearrange("a r n -> r a n").bitcast(I32),
            )
        for q in range(4):
            nc.gpsimd.dma_start(brow[32 * q : 32 * q + MT, :], b.rearrange("(m q i) -> q m i", q=4, i=32)[q, :, :])
        load_dw(0, 0, M)
        nc.sync.dma_start(offsets[:], offs)
        load_words(0)
        nc.sync.dma_start(w4[:].bitcast(I32), w4_words.rearrange("a p n -> p a n").bitcast(I32))
        load_dw(1, 0, M)
        load_words(1)
        load_words(2)

        def shift(engine, a):
            for q in range(4):
                engine.dma_start(
                    gs[32 * q : 32 * q + 4, a - 1, :].bitcast(I32),
                    gp[32 * q + 4 * a : 32 * q + 4 * a + 4, :].bitcast(I32),
                )

        nc.vector.tensor_copy(gp[:], tabs[:].indirect(offsets[:]))
        shift(nc.scalar, 1)
        shift(nc.gpsimd, 2)
        shift(nc.gpsimd, 3)
        load_words(3)
        load_dw(2, 0, 256)
        load_dw(3, 0, 256)
        load_dw(2, 256, 512)
        load_dw(3, 256, 384)
        load_dw(3, 384, 512)

        acc = [psum.tile([P, S], F32, name=f"acc{m}") for m in range(MT)]
        dq = [keep.tile([P, M], U32, name=f"dq{a}", align_bytes=64) for a in range(PASSES)]
        ds = [keep.tile([P, M], U8, name=f"ds{a}", align_bytes=64) for a in range(PASSES)]
        bf = [keep.tile([P, M, 4], BF16, name=f"bf{a}", align_bytes=64) for a in range(PASSES)]
        gw = [keep.tile([P, S], U32, name=f"gw{a}", align_bytes=64) for a in range(PASSES)]

        def interleave(engine_copy, a, c0, c1):
            engine_copy(bf[a][:, c0:c1, :], raw[a][:, :, c0:c1].rearrange("p j n -> p n j"))

        def quantize(a, c0, c1):
            nc.vector.quantize_mx(
                out=dq[a][:, c0:c1].bitcast(FP8X4),
                scales=ds[a][:, c0:c1],
                in_=bf[a][:, c0:c1, :].rearrange("p n j -> p (n j)"),
            )

        def base_passes(a):
            for m in range(MT):
                nc.tensor.matmul_mx(
                    out=acc[m][:],
                    lhsT=w4[:, a, 256 * m : 256 * (m + 1)].bitcast(FP4X4),
                    lhsT_scale=w4s[:, a, P * m : P * (m + 1)],
                    rhs=gw[a][:].bitcast(FP8X4),
                    rhs_scale=gp[:] if a == 0 else gs[:, a - 1, :],
                    start=(a == 0),
                    stop=False,
                )

        def change_passes(a, ms):
            for m in ms:
                nc.tensor.matmul_mx(
                    out=acc[m][:],
                    lhsT=dq[a][:, P * m : P * (m + 1)].bitcast(FP8X4),
                    lhsT_scale=ds[a][:, P * m : P * (m + 1)],
                    rhs=gw[a][:].bitcast(FP8X4),
                    rhs_scale=gp[4 * a : P, :],
                    start=False,
                    stop=(a == PASSES - 1),
                )

        def finish(m):
            res = keep.tile([P, S], F32, name=f"res{m}")
            nc.scalar.activation(res[:], acc[m][:], GELU, bias=bias[:, m : m + 1])
            nc.sync.dma_start(out[P * m : P * (m + 1), :], res[:])

        def gather_words(a):
            nc.vector.tensor_copy(gw[a][:], words[a][:].bitcast(U32).indirect(offsets[:]))

        interleave(nc.scalar.copy, 0, 0, M)
        gather_words(0)
        base_passes(0)
        quantize(0, 0, M)
        change_passes(0, range(MT))

        interleave(nc.scalar.copy, 1, 0, M)
        nc.vector.transpose(bias[:], brow[:])

        gather_words(1)
        quantize(1, 0, M)
        change_passes(1, range(MT))
        base_passes(1)
        gather_words(2)
        base_passes(2)
        gather_words(3)
        base_passes(3)

        for a, c0, c1, cut in TAIL:
            if cut > c0:
                interleave(nc.scalar.copy, a, c0, cut)
            interleave(nc.vector.tensor_copy, a, cut, c1)
            quantize(a, c0, c1)
            if (a, c0) == (2, 256):
                finish(0)
                finish(1)
            ms = range(c0 // P, c1 // P)
            change_passes(a, ms)
            if a == PASSES - 1 and c0 >= 256:
                for m in ms:
                    finish(m)
